import numpy as np
import ml_dtypes


def mxq(x, axis, fmt="e4m3"):
    dtype, down = {"e4m3": (ml_dtypes.float8_e4m3fn, 7), "e5m2": (ml_dtypes.float8_e5m2, 14)}[fmt]
    v = np.moveaxis(np.asarray(x, np.float32).astype(ml_dtypes.bfloat16).astype(np.float64), axis, -1)
    blocks = v.reshape(v.shape[:-1] + (-1, 32))
    amax = np.abs(blocks).max(-1, keepdims=True)
    byte = np.maximum(np.where(amax > 0, np.frexp(amax)[1] - 1 + 127, 0) - down, 1)
    scale = np.exp2(byte - 127.0)
    codes = (blocks / scale).astype(np.float32).astype(dtype).astype(np.float64)
    return np.moveaxis((codes * scale).reshape(v.shape), -1, axis)


WIDE = False


def mx_kscale(k):
    if not WIDE:
        return np.ones(k)
    levels = np.array([10, -10, 5, -5, 0])
    if k % 512:
        return np.exp2(np.random.permutation(np.resize(levels, k // 32))).repeat(32)
    a = np.empty((k // 512, 16))
    for p in range(k // 512):
        a[p, :8] = np.random.permutation(np.resize(levels, 8))
        for g in range(8):
            far = levels[np.abs(levels - a[p, g]) >= 10]
            a[p, g + 8] = far[np.random.randint(len(far))]
    return np.exp2(a.ravel()).repeat(32)


def f64(x):
    return np.asarray(x).astype(np.float64)


E2M1 = np.array([0.0, 0.5, 1.0, 1.5, 2.0, 3.0, 4.0, 6.0, -0.0, -0.5, -1.0, -1.5, -2.0, -3.0, -4.0, -6.0])


def pack_weight(w, fmt):
    k, n = w.shape
    w = f64(np.asarray(w, np.float32).astype(ml_dtypes.bfloat16)).reshape(k // 32, 32, n)
    amax = np.abs(w).max(1)
    if fmt == "e4m3":
        byte = np.frexp(amax)[1] - 1 + 127 - 7
    else:
        mant, ex = np.frexp(amax / 6.0)
        byte = np.where(mant > 0.5, ex, ex - 1) + 127
    byte = np.clip(np.where(amax > 0, byte, 1), 1, 254)
    scaled = (w * np.exp2(127.0 - byte)[:, None, :]).reshape(k, n).astype(np.float32)
    by_word = np.ascontiguousarray(scaled.reshape(k // 512, 128, 4, n).transpose(0, 1, 3, 2))
    if fmt == "e4m3":
        words = by_word.astype(ml_dtypes.float8_e4m3fn).view(np.uint8)
    else:
        c = by_word.astype(ml_dtypes.float4_e2m1fn).view(np.uint8) & 0xF
        words = (c[..., 0::2] | (c[..., 1::2] << 4)).reshape(k // 512, 128, 2 * n)
    return np.ascontiguousarray(words), np.ascontiguousarray(byte.astype(np.uint8).reshape(k // 512, 16, n))


def unpack_weight(words, scales, fmt):
    g, _, n = scales.shape
    words = np.ascontiguousarray(words).reshape(g, 128, n, -1)
    if fmt == "e4m3":
        vals = words.view(ml_dtypes.float8_e4m3fn).astype(np.float64)
    else:
        nib = np.empty((g, 128, n, 4), np.uint8)
        nib[..., 0::2] = words & 0xF
        nib[..., 1::2] = words >> 4
        vals = E2M1[nib]
    vals = vals * np.repeat(np.exp2(scales.astype(np.float64) - 127.0), 8, axis=1)[..., None]
    return vals.transpose(0, 1, 3, 2).reshape(g * 512, n)


def planes(y):
    n, m = y.shape
    v = y.astype(np.float32).astype(ml_dtypes.bfloat16).astype(np.float64).reshape(n // 32, 32, m)
    top = np.abs(v).max(1)
    byte = np.clip(np.where(top > 0, np.frexp(top)[1] - 1 + 127 - 7, 1), 1, 254)
    codes = (v * np.exp2(127.0 - byte)[:, None, :]).reshape(n, m).astype(np.float32).astype(ml_dtypes.float8_e4m3fn).view(np.uint8)
    words = codes.reshape(n // 512, 128, 4, m).transpose(0, 1, 3, 2)
    return np.ascontiguousarray(words), np.ascontiguousarray(byte.astype(np.uint8).reshape(n // 512, 16, m))


def gelu(v):
    return 0.5 * v * (1.0 + np.tanh(np.sqrt(2.0 / np.pi) * (v + 0.044715 * v**3)))


D, K, M, T = 128, 1024, 1536, 512


def setup_inputs():
    n = np.random.standard_normal
    s = mx_kscale(K)[:, None]
    p_w0 = pack_weight(n((K, M)) / np.sqrt(K) / s, "e2m1")
    p_w1 = pack_weight(n((K, M)) / np.sqrt(K) / s, "e4m3")
    return {
        "x": (n((K, T + 2 * D)) * s).astype(np.float32),
        "w0_words": p_w0[0],
        "w0_scales": p_w0[1],
        "w1_words": p_w1[0],
        "w1_scales": p_w1[1],
        "w2": (n((K, M)) / np.sqrt(K) / s).astype(np.float32),
        "b": (0.3 * n(1536)).astype(np.float32),
    }


def reference(x, w0_words, w0_scales, w1_words, w1_scales, w2, b):
    x_ = mxq(f64(x), 0, "e4m3")
    w0_ = unpack_weight(w0_words, w0_scales, "e2m1")
    w1_ = unpack_weight(w1_words, w1_scales, "e4m3")
    w2_ = mxq(f64(w2), 0, "e4m3")
    y = w0_.T @ x_[:, :T] + w1_.T @ x_[:, D:D + T] + w2_.T @ x_[:, 2 * D:]
    out_0 = gelu(y + f64(b)[:, None])
    return (out_0,) + planes(out_0)

@@ -1,0 +1,300 @@
+from contextlib import ExitStack
+
+import concourse.mybir as mybir
+
+D, K, M, T = 128, 1024, 1536, 512
+TX = T + 2 * D
+FLOPS = 2 * 3 * K * M * T
+
+F32 = mybir.dt.float32
+BF16 = mybir.dt.bfloat16
+I32 = mybir.dt.int32
+U8 = mybir.dt.uint8
+FP8X4 = mybir.dt.float8_e4m3fn_x4
+FP4X4 = mybir.dt.float4_e2m1fn_x4
+GELU = mybir.ActivationFunctionType.Gelu_apprx_tanh
+
+P = 128
+PACK = 4
+KP = P * PACK
+PASSES = K // KP
+GROUPS = M // KP
+W1_ROW = 4
+X_SPLIT = 320
+
+
+def tile_mix_dconv_fm_pl_gelu_kernel(
+    tc, x, w0_words, w0_scales, w1_words, w1_scales, w2, b, out_0, out_1, out_2
+):
+    nc = tc.nc
+    passes = range(PASSES)
+    groups = range(GROUPS)
+
+    with ExitStack() as ctx:
+        keep = ctx.enter_context(tc.tile_pool(name="keep", bufs=1))
+        stage = ctx.enter_context(tc.tile_pool(name="stage", bufs=4))
+        psum = ctx.enter_context(tc.psum_pool(name="psum", bufs=1))
+        ctx.enter_context(tc.manual_schedule())
+
+        def tiles(stem, shape, dtype, *counts):
+            made = {}
+            if len(counts) == 1:
+                keys = [(i,) for i in range(counts[0])]
+            else:
+                keys = [(i, j) for i in range(counts[0]) for j in range(counts[1])]
+            for key in keys:
+                label = stem + "".join("_%d" % i for i in key)
+                made[key] = keep.tile(shape, dtype, name=label, align_bytes=64)
+            return made
+
+        x_raw = tiles("x_raw", [P, PACK, TX], F32, PASSES)
+        x_bf = tiles("x_bf", [P, TX * PACK], BF16, PASSES)
+        x_codes = tiles("x_codes", [P, TX], I32, PASSES)
+        x_scales = tiles("x_scales", [P, TX], U8, PASSES)
+        w0_raw = tiles("w0_raw", [P, 2 * M], U8, PASSES)
+        w0_codes = tiles("w0_codes", [P, 2 * KP], U8, PASSES, GROUPS)
+        w1_raw = tiles("w1_raw", [P, M], I32, PASSES)
+        w1_codes = tiles("w1_codes", [P, KP], I32, PASSES, GROUPS)
+        w01_scales = tiles("w01_scales", [P, M], U8, PASSES + 1)
+        w2_raw = tiles("w2_raw", [P, PACK, KP], F32, PASSES, GROUPS)
+        w2_codes = tiles("w2_codes", [P, KP], I32, PASSES, GROUPS)
+        w2_scales = tiles("w2_scales", [P, KP], U8, PASSES, GROUPS)
+        y = tiles("y", [P, PACK, T], F32, GROUPS)
+        y_bf = tiles("y_bf", [P, T * PACK], BF16, GROUPS)
+        y_codes = tiles("y_codes", [P, T], I32, GROUPS)
+        y_scales = keep.tile([P, GROUPS, T], U8, name="y_scales", align_bytes=64)
+        scales_raw = keep.tile([P, PASSES + 1, M], U8, name="scales_raw", align_bytes=64)
+        bias = keep.tile([P, GROUPS, PACK], F32, name="bias")
+        warm = keep.tile([P, 1], F32, name="warm")
+        w2_bf = {}
+        acc = {}
+
+        def load_x(g):
+            nc.sync.dma_start(out=x_raw[g,][:], in_=x[g * KP : (g + 1) * KP, :].rearrange("(p j) t -> p j t", j=PACK))
+
+        def load_w0(g):
+            nc.sync.dma_start(out=w0_raw[g,][:].bitcast(I32), in_=w0_words[g].bitcast(I32))
+
+        def load_w1(g):
+            nc.sync.dma_start(out=w1_raw[g,][:], in_=w1_words[g].rearrange("p n i -> p (n i)").bitcast(I32))
+
+        def load_w2(g, a):
+            rows = w2[g * KP : (g + 1) * KP, a * KP : (a + 1) * KP]
+            nc.sync.dma_start(out=w2_raw[g, a][:], in_=rows.rearrange("(p j) n -> p j n", j=PACK))
+
+        def load_scales(engine, src, row, slot):
+            for q in range(4):
+                engine.dma_start(
+                    out=scales_raw[32 * q + row : 32 * q + row + 4, slot : slot + PASSES, :].bitcast(I32),
+                    in_=src[:, 4 * q : 4 * q + 4, :].rearrange("g r n -> r g n").bitcast(I32),
+                )
+
+        nc.vector.memset(scales_raw[:].rearrange("p g n -> p (g n)").bitcast(I32), 0)
+        nc.scalar.dma_start(out=bias[:], in_=b.rearrange("(a p r) -> p a r", a=GROUPS, r=PACK))
+        nc.scalar.activation(out=warm[:], in_=bias[:, 0, 0:1], func=GELU)
+        load_x(0)
+        load_scales(nc.sync, w0_scales, 0, 0)
+        load_w0(0)
+        load_w1(0)
+        load_scales(nc.sync, w1_scales, W1_ROW, 1)
+        load_x(1)
+        load_w0(1)
+        load_w1(1)
+        for a in groups:
+            for g in passes:
+                load_w2(g, a)
+
+        def deal_w0(g, a):
+            nc.vector.tensor_copy(
+                out=w0_codes[g, a][:].rearrange("p (r m c) -> p r m c", r=PACK, c=2),
+                in_=w0_raw[g,][:, 2 * KP * a : 2 * KP * (a + 1)].rearrange("p (m r c) -> p r m c", r=PACK, c=2),
+            )
+
+        def deal_w1(g, a):
+            nc.vector.tensor_copy(
+                out=w1_codes[g, a][:].rearrange("p (h r m) -> p h m r", h=2, r=2),
+                in_=w1_raw[g,][:, KP * a : KP * (a + 1)].rearrange("p (m h r) -> p h m r", h=2, r=2),
+            )
+
+        def deal_scales(g, lo, hi):
+            cols = slice(KP * lo, KP * hi)
+            nc.vector.tensor_copy(
+                out=w01_scales[g,][:, cols].rearrange("p (a r m) -> p a r m", a=hi - lo, r=PACK),
+                in_=scales_raw[:, g, cols].rearrange("p (a m r) -> p a r m", a=hi - lo, r=PACK),
+            )
+
+        def interleave(copy, dst, src, lo, hi):
+            copy(
+                out=dst[:, PACK * lo : PACK * hi].rearrange("p (c i j) -> p c j i", i=4, j=PACK),
+                in_=src[:, :, lo:hi].rearrange("p j (c i) -> p c j i", i=4),
+            )
+
+        def quantize(codes, scales, src, lo, hi):
+            nc.vector.quantize_mx(out=codes[:, lo:hi].bitcast(FP8X4), scales=scales[:, lo:hi], in_=src[:, PACK * lo : PACK * hi])
+
+        def cast_x(g):
+            interleave(nc.vector.tensor_copy, x_bf[g,], x_raw[g,], 0, X_SPLIT)
+            interleave(nc.scalar.copy, x_bf[g,], x_raw[g,], X_SPLIT, T)
+            interleave(nc.scalar.copy, x_bf[g,], x_raw[g,], T, TX)
+
+        def quantize_x(g, lo, hi):
+            quantize(x_codes[g,], x_scales[g,], x_bf[g,], lo, hi)
+
+        def cast_w2(copy, g, a, h):
+            w2_bf[g, a, h] = stage.tile([P, 2 * KP], BF16, name="w2_bf", align_bytes=64)
+            copy(
+                out=w2_bf[g, a, h][:].rearrange("p (r m j) -> p m j r", r=2, j=PACK),
+                in_=w2_raw[g, a][:].rearrange("p j (m h r) -> p h m j r", h=2, r=2)[:, h, :, :, :],
+            )
+
+        def quantize_w2(g, a, h):
+            cols = slice(2 * P * h, 2 * P * (h + 1))
+            nc.vector.quantize_mx(
+                out=w2_codes[g, a][:, cols].bitcast(FP8X4), scales=w2_scales[g, a][:, cols], in_=w2_bf[g, a, h][:]
+            )
+
+        def matmul(tap, g, a, r):
+            first = tap == 0 and g == 0
+            if first:
+                acc[a, r] = psum.tile([P, T], F32, name="acc", tag="bank%d" % (PACK * (a % 2) + r))
+            cols = slice(P * r, P * (r + 1))
+            plane = slice(KP * a + P * r, KP * a + P * (r + 1))
+            if tap == 0:
+                lhs = w0_codes[g, a][:, 2 * P * r : 2 * P * (r + 1)].bitcast(FP4X4)
+                lhs_scale = w01_scales[g,][:, plane]
+            elif tap == 1:
+                lhs = w1_codes[g, a][:, cols].bitcast(FP8X4)
+                lhs_scale = w01_scales[g + 1,][W1_ROW:P, plane]
+            else:
+                lhs = w2_codes[g, a][:, cols].bitcast(FP8X4)
+                lhs_scale = w2_scales[g, a][:, cols]
+            window = slice(tap * D, tap * D + T)
+            nc.tensor.matmul_mx(
+                out=acc[a, r][:],
+                lhsT=lhs,
+                lhsT_scale=lhs_scale,
+                rhs=x_codes[g,][:, window].bitcast(FP8X4),
+                rhs_scale=x_scales[g,][:, window],
+                start=first,
+                stop=(tap == 2 and g == PASSES - 1),
+            )
+
+        def matmuls(tap, g, *which):
+            for a in which:
+                for r in range(PACK):
+                    matmul(tap, g, a, r)
+
+        def gelu(a, r):
+            nc.scalar.activation(out=y[a,][:, r, :], in_=acc[a, r][:], func=GELU, bias=bias[:, a, r : r + 1])
+
+        def cast_y(a, h):
+            interleave(nc.vector.tensor_copy, y_bf[a,], y[a,], h * T // 2, (h + 1) * T // 2)
+
+        def quantize_y(a):
+            quantize(y_codes[a,], y_scales[:, a, :], y_bf[a,], 0, T)
+
+        def store_y(a, lo, hi):
+            rows = out_0[a * KP : (a + 1) * KP, :].rearrange("(p r) t -> p r t", r=PACK)
+            nc.sync.dma_start(out=rows[:, lo:hi, :], in_=y[a,][:, lo:hi, :])
+
+        def store_codes(a):
+            nc.sync.dma_start(out=out_1[a].rearrange("p t i -> p (t i)").bitcast(I32), in_=y_codes[a,][:])
+
+        def store_scales():
+            for q in range(4):
+                nc.scalar.dma_start(
+                    out=out_2[:, 4 * q : 4 * q + 4, :].rearrange("a r t -> r a t").bitcast(I32),
+                    in_=y_scales[32 * q : 32 * q + 4, :, :].bitcast(I32),
+                )
+
+        vec, act = nc.vector.tensor_copy, nc.scalar.copy
+
+        cast_x(0)
+        deal_scales(0, 0, 2)
+        quantize_x(0, 0, T)
+        deal_w0(0, 0)
+        deal_w0(0, 1)
+        matmuls(0, 0, 0, 1)
+        quantize_x(0, T, TX)
+        deal_w1(0, 0)
+        deal_scales(1, 0, 2)
+        deal_w1(0, 1)
+        matmuls(1, 0, 0, 1)
+        deal_w0(0, 2)
+        deal_w1(0, 2)
+        deal_scales(2, 0, 2)
+
+        cast_x(1)
+        deal_w0(1, 0)
+        quantize_x(1, 0, T)
+        deal_w0(1, 1)
+        matmuls(0, 1, 0, 1)
+        quantize_x(1, T, TX)
+        deal_w1(1, 0)
+        deal_w1(1, 1)
+        matmuls(1, 1, 0, 1)
+        deal_w0(1, 2)
+        deal_w1(1, 2)
+        for slot in range(PASSES + 1):
+            deal_scales(slot, 2, 3)
+
+        for g in passes:
+            cast_w2(vec, g, 0, 0)
+            cast_w2(act, g, 0, 1)
+            quantize_w2(g, 0, 0)
+            quantize_w2(g, 0, 1)
+            matmuls(2, g, 0)
+
+        cast_w2(vec, 0, 1, 0)
+        cast_w2(vec, 0, 1, 1)
+        quantize_w2(0, 1, 0)
+        quantize_w2(0, 1, 1)
+        for r in range(PACK):
+            gelu(0, r)
+            for g in passes:
+                for tap in (0, 1):
+                    matmul(tap, g, 2, r)
+            if r == 1:
+                matmuls(2, 0, 1)
+        store_y(0, 0, PACK)
+
+        cast_y(0, 0)
+        cast_w2(vec, 1, 1, 0)
+        cast_w2(act, 1, 1, 1)
+        cast_y(0, 1)
+        quantize_w2(1, 1, 0)
+        quantize_w2(1, 1, 1)
+        matmuls(2, 1, 1)
+        quantize_y(0)
+        store_codes(0)
+
+        cast_w2(vec, 0, 2, 0)
+        cast_w2(act, 0, 2, 1)
+        quantize_w2(0, 2, 0)
+        quantize_w2(0, 2, 1)
+        matmuls(2, 0, 2)
+        for r in range(PACK):
+            gelu(1, r)
+        store_y(1, 0, PACK)
+
+        cast_w2(vec, 1, 2, 0)
+        cast_w2(vec, 1, 2, 1)
+        quantize_w2(1, 2, 0)
+        quantize_w2(1, 2, 1)
+        matmuls(2, 1, 2)
+        cast_y(1, 0)
+        cast_y(1, 1)
+        quantize_y(1)
+        for r in range(PACK):
+            gelu(2, r)
+            if r == 1:
+                store_y(2, 0, 2)
+                store_codes(1)
+        store_y(2, 2, PACK)
+        interleave(vec, y_bf[2,], y[2,], 0, 256)
+        interleave(act, y_bf[2,], y[2,], 384, 512)
+        interleave(vec, y_bf[2,], y[2,], 256, 384)
+        quantize(y_codes[2,], y_scales[:, 2, :], y_bf[2,], 0, 256)
+        quantize(y_codes[2,], y_scales[:, 2, :], y_bf[2,], 256, 512)
+        store_codes(2)
+        store_scales()

@@ -55,7 +55,7 @@ def tile_mix_dconv_fm_pl_gelu_kernel(
         w0_codes = tiles("w0_codes", [P, 2 * KP], U8, PASSES, GROUPS)
         w1_raw = tiles("w1_raw", [P, M], I32, PASSES)
         w1_codes = tiles("w1_codes", [P, KP], I32, PASSES, GROUPS)
-        w01_scales = tiles("w01_scales", [P, M], U8, PASSES + 1)
+        w01_scales = tiles("w01_scales", [P, M], U8, PASSES)
         w2_raw = tiles("w2_raw", [P, PACK, KP], F32, PASSES, GROUPS)
         w2_codes = tiles("w2_codes", [P, KP], I32, PASSES, GROUPS)
         w2_scales = tiles("w2_scales", [P, KP], U8, PASSES, GROUPS)
@@ -63,7 +63,7 @@ def tile_mix_dconv_fm_pl_gelu_kernel(
         y_bf = tiles("y_bf", [P, T * PACK], BF16, GROUPS)
         y_codes = tiles("y_codes", [P, T], I32, GROUPS)
         y_scales = keep.tile([P, GROUPS, T], U8, name="y_scales", align_bytes=64)
-        scales_raw = keep.tile([P, PASSES + 1, M], U8, name="scales_raw", align_bytes=64)
+        scales_raw = keep.tile([P, PASSES, M], U8, name="scales_raw", align_bytes=64)
         bias = keep.tile([P, GROUPS, PACK], F32, name="bias")
         warm = keep.tile([P, 1], F32, name="warm")
         w2_bf = {}
@@ -82,21 +82,21 @@ def tile_mix_dconv_fm_pl_gelu_kernel(
             rows = w2[g * KP : (g + 1) * KP, a * KP : (a + 1) * KP]
             nc.sync.dma_start(out=w2_raw[g, a][:], in_=rows.rearrange("(p j) n -> p j n", j=PACK))
 
-        def load_scales(engine, src, row, slot):
-            for q in range(4):
+        def load_scales(engine, src, row):
+            for r in range(4):
                 engine.dma_start(
-                    out=scales_raw[32 * q + row : 32 * q + row + 4, slot : slot + PASSES, :].bitcast(I32),
-                    in_=src[:, 4 * q : 4 * q + 4, :].rearrange("g r n -> r g n").bitcast(I32),
+                    out=scales_raw[row + r : P : 32, :, :].bitcast(I32),
+                    in_=src.rearrange("g (q r) n -> r q g n", r=4)[r].bitcast(I32),
                 )
 
         nc.vector.memset(scales_raw[:].rearrange("p g n -> p (g n)").bitcast(I32), 0)
         nc.scalar.dma_start(out=bias[:], in_=b.rearrange("(a p r) -> p a r", a=GROUPS, r=PACK))
         nc.scalar.activation(out=warm[:], in_=bias[:, 0, 0:1], func=GELU)
+        load_scales(nc.gpsimd, w1_scales, W1_ROW)
         load_x(0)
-        load_scales(nc.sync, w0_scales, 0, 0)
+        load_scales(nc.sync, w0_scales, 0)
         load_w0(0)
         load_w1(0)
-        load_scales(nc.sync, w1_scales, W1_ROW, 1)
         load_x(1)
         load_w0(1)
         load_w1(1)
@@ -164,7 +164,7 @@ def tile_mix_dconv_fm_pl_gelu_kernel(
                 lhs_scale = w01_scales[g,][:, plane]
             elif tap == 1:
                 lhs = w1_codes[g, a][:, cols].bitcast(FP8X4)
-                lhs_scale = w01_scales[g + 1,][W1_ROW:P, plane]
+                lhs_scale = w01_scales[g,][W1_ROW:P, plane]
             else:
                 lhs = w2_codes[g, a][:, cols].bitcast(FP8X4)
                 lhs_scale = w2_scales[g, a][:, cols]
@@ -201,28 +201,27 @@ def tile_mix_dconv_fm_pl_gelu_kernel(
             nc.sync.dma_start(out=out_1[a].rearrange("p t i -> p (t i)").bitcast(I32), in_=y_codes[a,][:])
 
         def store_scales():
-            for q in range(4):
+            for r in range(4):
                 nc.scalar.dma_start(
-                    out=out_2[:, 4 * q : 4 * q + 4, :].rearrange("a r t -> r a t").bitcast(I32),
-                    in_=y_scales[32 * q : 32 * q + 4, :, :].bitcast(I32),
+                    out=out_2.rearrange("a (q r) t -> r q a t", r=4)[r].bitcast(I32),
+                    in_=y_scales[r:P:32, :, :].bitcast(I32),
                 )
 
         vec, act = nc.vector.tensor_copy, nc.scalar.copy
 
         cast_x(0)
-        deal_scales(0, 0, 2)
         quantize_x(0, 0, T)
+        deal_scales(0, 0, 2)
         deal_w0(0, 0)
         deal_w0(0, 1)
         matmuls(0, 0, 0, 1)
         quantize_x(0, T, TX)
         deal_w1(0, 0)
-        deal_scales(1, 0, 2)
         deal_w1(0, 1)
         matmuls(1, 0, 0, 1)
         deal_w0(0, 2)
         deal_w1(0, 2)
-        deal_scales(2, 0, 2)
+        deal_scales(1, 0, 2)
 
         cast_x(1)
         deal_w0(1, 0)
@@ -235,8 +234,8 @@ def tile_mix_dconv_fm_pl_gelu_kernel(
         matmuls(1, 1, 0, 1)
         deal_w0(1, 2)
         deal_w1(1, 2)
-        for slot in range(PASSES + 1):
-            deal_scales(slot, 2, 3)
+        for g in passes:
+            deal_scales(g, 2, 3)
 
         for g in passes:
             cast_w2(vec, g, 0, 0)

@@ -82,20 +82,21 @@ def tile_mix_dconv_fm_pl_gelu_kernel(
             rows = w2[g * KP : (g + 1) * KP, a * KP : (a + 1) * KP]
             nc.sync.dma_start(out=w2_raw[g, a][:], in_=rows.rearrange("(p j) n -> p j n", j=PACK))
 
-        def load_scales(engine, src, row):
-            for r in range(4):
-                engine.dma_start(
-                    out=scales_raw[row + r : P : 32, :, :].bitcast(I32),
-                    in_=src.rearrange("g (q r) n -> r q g n", r=4)[r].bitcast(I32),
-                )
+        def load_scales(*rows):
+            for r in rows:
+                for src, first in ((w0_scales, 0), (w1_scales, W1_ROW)):
+                    nc.sync.dma_start(
+                        out=scales_raw[first + r : P : 32, :, :].bitcast(I32),
+                        in_=src.rearrange("g (q r) n -> r q g n", r=4)[r].bitcast(I32),
+                    )
 
         nc.vector.memset(scales_raw[:].rearrange("p g n -> p (g n)").bitcast(I32), 0)
         nc.scalar.dma_start(out=bias[:], in_=b.rearrange("(a p r) -> p a r", a=GROUPS, r=PACK))
         nc.scalar.activation(out=warm[:], in_=bias[:, 0, 0:1], func=GELU)
-        load_scales(nc.gpsimd, w1_scales, W1_ROW)
         load_x(0)
-        load_scales(nc.sync, w0_scales, 0)
+        load_scales(0, 1)
         load_w0(0)
+        load_scales(2, 3)
         load_w1(0)
         load_x(1)
         load_w0(1)
@@ -211,8 +212,8 @@ def tile_mix_dconv_fm_pl_gelu_kernel(
 
         cast_x(0)
         quantize_x(0, 0, T)
-        deal_scales(0, 0, 2)
         deal_w0(0, 0)
+        deal_scales(0, 0, 2)
         deal_w0(0, 1)
         matmuls(0, 0, 0, 1)
         quantize_x(0, T, TX)

@@ -47,13 +47,11 @@ def tile_mix_dconv_fm_pl_gelu_kernel(
                 made[key] = keep.tile(shape, dtype, name=label, align_bytes=64)
             return made
 
-        x_raw = tiles("x_raw", [P, PACK, TX], F32, PASSES)
         x_bf = tiles("x_bf", [P, TX * PACK], BF16, PASSES)
         x_codes = tiles("x_codes", [P, TX], I32, PASSES)
         x_scales = tiles("x_scales", [P, TX], U8, PASSES)
-        w0_raw = tiles("w0_raw", [P, 2 * M], U8, PASSES)
+        w0_raw, w1_raw, x_raw = {}, {}, {}
         w0_codes = tiles("w0_codes", [P, 2 * KP], U8, PASSES, GROUPS)
-        w1_raw = tiles("w1_raw", [P, M], I32, PASSES)
         w1_codes = tiles("w1_codes", [P, KP], I32, PASSES, GROUPS)
         w01_scales = tiles("w01_scales", [P, M], U8, PASSES)
         w2_raw = tiles("w2_raw", [P, PACK, KP], F32, PASSES, GROUPS)
@@ -69,14 +67,24 @@ def tile_mix_dconv_fm_pl_gelu_kernel(
         w2_bf = {}
         acc = {}
 
-        def load_x(g):
-            nc.sync.dma_start(out=x_raw[g,][:], in_=x[g * KP : (g + 1) * KP, :].rearrange("(p j) t -> p j t", j=PACK))
+        def load_x(g, lo, hi):
+            piece = keep.tile([P, PACK, hi - lo], F32, name="x_raw_%d_%d" % (g, lo), align_bytes=64)
+            nc.sync.dma_start(out=piece[:], in_=x[g * KP : (g + 1) * KP, lo:hi].rearrange("(p j) t -> p j t", j=PACK))
+            x_raw[g, lo] = piece
 
-        def load_w0(g):
-            nc.sync.dma_start(out=w0_raw[g,][:].bitcast(I32), in_=w0_words[g].bitcast(I32))
+        def load_words(held, src, stem, gs, lo, hi):
+            width = src.shape[2] // GROUPS
+            piece = keep.tile([P, len(gs), width * (hi - lo)], I32, name="%s_%d_%d" % (stem, gs[0], lo), align_bytes=64)
+            nc.sync.dma_start(out=piece[:], in_=src[:, gs[0] : gs[-1] + 1, width * lo : width * hi])
+            for i, g in enumerate(gs):
+                for a in range(lo, hi):
+                    held[g, a] = piece[:, i, width * (a - lo) : width * (a - lo + 1)]
 
-        def load_w1(g):
-            nc.sync.dma_start(out=w1_raw[g,][:], in_=w1_words[g].rearrange("p n i -> p (n i)").bitcast(I32))
+        def load_w0(gs, lo, hi):
+            load_words(w0_raw, w0_words.bitcast(I32).rearrange("g p c -> p g c"), "w0_raw", gs, lo, hi)
+
+        def load_w1(gs, lo, hi):
+            load_words(w1_raw, w1_words.rearrange("g p n i -> p g (n i)").bitcast(I32), "w1_raw", gs, lo, hi)
 
         def load_w2(g, a):
             rows = w2[g * KP : (g + 1) * KP, a * KP : (a + 1) * KP]
@@ -91,30 +99,35 @@ def tile_mix_dconv_fm_pl_gelu_kernel(
                     )
 
         nc.vector.memset(scales_raw[:].rearrange("p g n -> p (g n)").bitcast(I32), 0)
-        nc.scalar.dma_start(out=bias[:], in_=b.rearrange("(a p r) -> p a r", a=GROUPS, r=PACK))
-        nc.scalar.activation(out=warm[:], in_=bias[:, 0, 0:1], func=GELU)
-        load_x(0)
+        load_w0((0,), 0, 3)
         load_scales(0, 1)
-        load_w0(0)
+        load_x(0, 0, T)
         load_scales(2, 3)
-        load_w1(0)
-        load_x(1)
-        load_w0(1)
-        load_w1(1)
-        for a in groups:
+        load_x(0, T, TX)
+        load_w1((0,), 0, 2)
+        load_x(1, 0, TX)
+        load_w0((1,), 0, 3)
+        load_w1((1,), 0, 2)
+        nc.sync.dma_start(out=bias[:], in_=b.rearrange("(a p r) -> p a r", a=GROUPS, r=PACK))
+        load_w2(0, 0)
+        load_w2(1, 0)
+        load_w1((0,), 2, 3)
+        for a in (1, 2):
             for g in passes:
                 load_w2(g, a)
+        load_w1((1,), 2, 3)
+        nc.scalar.activation(out=warm[:], in_=x_raw[0, 0][:, 0, 0:1], func=GELU)
 
         def deal_w0(g, a):
             nc.vector.tensor_copy(
                 out=w0_codes[g, a][:].rearrange("p (r m c) -> p r m c", r=PACK, c=2),
-                in_=w0_raw[g,][:, 2 * KP * a : 2 * KP * (a + 1)].rearrange("p (m r c) -> p r m c", r=PACK, c=2),
+                in_=w0_raw[g, a].bitcast(U8).rearrange("p (m r c) -> p r m c", r=PACK, c=2),
             )
 
         def deal_w1(g, a):
             nc.vector.tensor_copy(
                 out=w1_codes[g, a][:].rearrange("p (h r m) -> p h m r", h=2, r=2),
-                in_=w1_raw[g,][:, KP * a : KP * (a + 1)].rearrange("p (m h r) -> p h m r", h=2, r=2),
+                in_=w1_raw[g, a].rearrange("p (m h r) -> p h m r", h=2, r=2),
             )
 
         def deal_scales(g, lo, hi):
@@ -124,19 +137,22 @@ def tile_mix_dconv_fm_pl_gelu_kernel(
                 in_=scales_raw[:, g, cols].rearrange("p (a m r) -> p a r m", a=hi - lo, r=PACK),
             )
 
-        def interleave(copy, dst, src, lo, hi):
+        def interleave(copy, dst, src, lo, hi, first=0):
             copy(
                 out=dst[:, PACK * lo : PACK * hi].rearrange("p (c i j) -> p c j i", i=4, j=PACK),
-                in_=src[:, :, lo:hi].rearrange("p j (c i) -> p c j i", i=4),
+                in_=src[:, :, lo - first : hi - first].rearrange("p j (c i) -> p c j i", i=4),
             )
 
         def quantize(codes, scales, src, lo, hi):
             nc.vector.quantize_mx(out=codes[:, lo:hi].bitcast(FP8X4), scales=scales[:, lo:hi], in_=src[:, PACK * lo : PACK * hi])
 
         def cast_x(g):
-            interleave(nc.vector.tensor_copy, x_bf[g,], x_raw[g,], 0, X_SPLIT)
-            interleave(nc.scalar.copy, x_bf[g,], x_raw[g,], X_SPLIT, T)
-            interleave(nc.scalar.copy, x_bf[g,], x_raw[g,], T, TX)
+            interleave(nc.vector.tensor_copy, x_bf[g,], x_raw[g, 0], 0, X_SPLIT)
+            interleave(nc.scalar.copy, x_bf[g,], x_raw[g, 0], X_SPLIT, T)
+            if g == 0:
+                interleave(nc.scalar.copy, x_bf[g,], x_raw[g, T], T, TX, T)
+            else:
+                interleave(nc.scalar.copy, x_bf[g,], x_raw[g, 0], T, TX)
 
         def quantize_x(g, lo, hi):
             quantize(x_codes[g,], x_scales[g,], x_bf[g,], lo, hi)
@@ -185,11 +201,11 @@ def tile_mix_dconv_fm_pl_gelu_kernel(
                 for r in range(PACK):
                     matmul(tap, g, a, r)
 
-        def gelu(a, r):
-            nc.scalar.activation(out=y[a,][:, r, :], in_=acc[a, r][:], func=GELU, bias=bias[:, a, r : r + 1])
+        def gelu(a, r, lo, hi):
+            nc.scalar.activation(out=y[a,][:, r, lo:hi], in_=acc[a, r][:, lo:hi], func=GELU, bias=bias[:, a, r : r + 1])
 
-        def cast_y(a, h):
-            interleave(nc.vector.tensor_copy, y_bf[a,], y[a,], h * T // 2, (h + 1) * T // 2)
+        def cast_y(copy, a, lo, hi):
+            interleave(copy, y_bf[a,], y[a,], lo, hi)
 
         def quantize_y(a):
             quantize(y_codes[a,], y_scales[:, a, :], y_bf[a,], 0, T)
@@ -210,19 +226,20 @@ def tile_mix_dconv_fm_pl_gelu_kernel(
 
         vec, act = nc.vector.tensor_copy, nc.scalar.copy
 
+        for a in groups:
+            deal_w0(0, a)
         cast_x(0)
+        deal_scales(0, 0, 1)
         quantize_x(0, 0, T)
-        deal_w0(0, 0)
-        deal_scales(0, 0, 2)
-        deal_w0(0, 1)
-        matmuls(0, 0, 0, 1)
+        matmuls(0, 0, 0)
+        deal_scales(0, 1, 2)
+        matmuls(0, 0, 1)
         quantize_x(0, T, TX)
         deal_w1(0, 0)
         deal_w1(0, 1)
         matmuls(1, 0, 0, 1)
-        deal_w0(0, 2)
-        deal_w1(0, 2)
-        deal_scales(1, 0, 2)
+        deal_scales(1, 0, 3)
+        deal_scales(0, 2, 3)
 
         cast_x(1)
         deal_w0(1, 0)
@@ -234,9 +251,6 @@ def tile_mix_dconv_fm_pl_gelu_kernel(
         deal_w1(1, 1)
         matmuls(1, 1, 0, 1)
         deal_w0(1, 2)
-        deal_w1(1, 2)
-        for g in passes:
-            deal_scales(g, 2, 3)
 
         for g in passes:
             cast_w2(vec, g, 0, 0)
@@ -244,57 +258,56 @@ def tile_mix_dconv_fm_pl_gelu_kernel(
             quantize_w2(g, 0, 0)
             quantize_w2(g, 0, 1)
             matmuls(2, g, 0)
+        deal_w1(0, 2)
+
+        for r in range(PACK):
+            gelu(0, r, 0, T)
+            for tap, g in ((0, 0), (0, 1), (1, 0)):
+                matmul(tap, g, 2, r)
+        store_y(0, 0, PACK)
 
         cast_w2(vec, 0, 1, 0)
         cast_w2(vec, 0, 1, 1)
         quantize_w2(0, 1, 0)
         quantize_w2(0, 1, 1)
-        for r in range(PACK):
-            gelu(0, r)
-            for g in passes:
-                for tap in (0, 1):
-                    matmul(tap, g, 2, r)
-            if r == 1:
-                matmuls(2, 0, 1)
-        store_y(0, 0, PACK)
-
-        cast_y(0, 0)
+        matmuls(2, 0, 1)
+        cast_y(vec, 0, 0, 256)
+        cast_y(act, 0, 256, T)
         cast_w2(vec, 1, 1, 0)
         cast_w2(act, 1, 1, 1)
-        cast_y(0, 1)
+        quantize_y(0)
         quantize_w2(1, 1, 0)
         quantize_w2(1, 1, 1)
         matmuls(2, 1, 1)
-        quantize_y(0)
         store_codes(0)
+        for r in range(PACK):
+            gelu(1, r, 0, T)
+        store_y(1, 0, PACK)
 
         cast_w2(vec, 0, 2, 0)
-        cast_w2(act, 0, 2, 1)
+        cast_w2(vec, 0, 2, 1)
         quantize_w2(0, 2, 0)
         quantize_w2(0, 2, 1)
         matmuls(2, 0, 2)
-        for r in range(PACK):
-            gelu(1, r)
-        store_y(1, 0, PACK)
-
         cast_w2(vec, 1, 2, 0)
-        cast_w2(vec, 1, 2, 1)
+        cast_w2(act, 1, 2, 1)
+        deal_w1(1, 2)
         quantize_w2(1, 2, 0)
         quantize_w2(1, 2, 1)
-        matmuls(2, 1, 2)
-        cast_y(1, 0)
-        cast_y(1, 1)
+        cast_y(vec, 1, 0, T)
         quantize_y(1)
         for r in range(PACK):
-            gelu(2, r)
+            matmul(1, 1, 2, r)
+            matmul(2, 1, 2, r)
+            gelu(2, r, 0, T)
             if r == 1:
                 store_y(2, 0, 2)
                 store_codes(1)
         store_y(2, 2, PACK)
-        interleave(vec, y_bf[2,], y[2,], 0, 256)
-        interleave(act, y_bf[2,], y[2,], 384, 512)
-        interleave(vec, y_bf[2,], y[2,], 256, 384)
+        cast_y(vec, 2, 0, 256)
+        cast_y(act, 2, 416, T)
+        cast_y(vec, 2, 256, 416)
         quantize(y_codes[2,], y_scales[:, 2, :], y_bf[2,], 0, 256)
-        quantize(y_codes[2,], y_scales[:, 2, :], y_bf[2,], 256, 512)
+        quantize(y_codes[2,], y_scales[:, 2, :], y_bf[2,], 256, T)
         store_codes(2)
         store_scales()

@@ -63,7 +63,6 @@ def tile_mix_dconv_fm_pl_gelu_kernel(
         y_scales = keep.tile([P, GROUPS, T], U8, name="y_scales", align_bytes=64)
         scales_raw = keep.tile([P, PASSES, M], U8, name="scales_raw", align_bytes=64)
         bias = keep.tile([P, GROUPS, PACK], F32, name="bias")
-        warm = keep.tile([P, 1], F32, name="warm")
         w2_bf = {}
         acc = {}
 
@@ -116,7 +115,6 @@ def tile_mix_dconv_fm_pl_gelu_kernel(
             for g in passes:
                 load_w2(g, a)
         load_w1((1,), 2, 3)
-        nc.scalar.activation(out=warm[:], in_=x_raw[0, 0][:, 0, 0:1], func=GELU)
 
         def deal_w0(g, a):
             nc.vector.tensor_copy(
@@ -252,33 +250,42 @@ def tile_mix_dconv_fm_pl_gelu_kernel(
         matmuls(1, 1, 0, 1)
         deal_w0(1, 2)
 
-        for g in passes:
-            cast_w2(vec, g, 0, 0)
-            cast_w2(act, g, 0, 1)
-            quantize_w2(g, 0, 0)
-            quantize_w2(g, 0, 1)
-            matmuls(2, g, 0)
+        cast_w2(act, 0, 0, 0)
+        cast_w2(act, 0, 0, 1)
+        quantize_w2(0, 0, 0)
+        cast_w2(vec, 1, 0, 0)
+        quantize_w2(0, 0, 1)
+        matmuls(2, 0, 0)
+        cast_w2(vec, 1, 0, 1)
+        quantize_w2(1, 0, 0)
+        quantize_w2(1, 0, 1)
+        matmuls(2, 1, 0)
         deal_w1(0, 2)
+
+        def early_taps(r):
+            for tap, g in ((0, 0), (0, 1), (1, 0)):
+                matmul(tap, g, 2, r)
 
         for r in range(PACK):
             gelu(0, r, 0, T)
-            for tap, g in ((0, 0), (0, 1), (1, 0)):
-                matmul(tap, g, 2, r)
         store_y(0, 0, PACK)
+        for r in range(PACK - 1):
+            early_taps(r)
 
         cast_w2(vec, 0, 1, 0)
         cast_w2(vec, 0, 1, 1)
         quantize_w2(0, 1, 0)
         quantize_w2(0, 1, 1)
         matmuls(2, 0, 1)
-        cast_y(vec, 0, 0, 256)
-        cast_y(act, 0, 256, T)
         cast_w2(vec, 1, 1, 0)
         cast_w2(act, 1, 1, 1)
-        quantize_y(0)
+        cast_y(vec, 0, 0, 320)
+        cast_y(act, 0, 320, T)
         quantize_w2(1, 1, 0)
         quantize_w2(1, 1, 1)
         matmuls(2, 1, 1)
+        early_taps(PACK - 1)
+        quantize_y(0)
         store_codes(0)
         for r in range(PACK):
             gelu(1, r, 0, T)

from contextlib import ExitStack

import concourse.mybir as mybir

D, K, M, T = 128, 1024, 1536, 512
TX = T + 2 * D
FLOPS = 2 * 3 * K * M * T

F32 = mybir.dt.float32
BF16 = mybir.dt.bfloat16
I32 = mybir.dt.int32
U8 = mybir.dt.uint8
FP8X4 = mybir.dt.float8_e4m3fn_x4
FP4X4 = mybir.dt.float4_e2m1fn_x4
GELU = mybir.ActivationFunctionType.Gelu_apprx_tanh

P = 128
PACK = 4
KP = P * PACK
PASSES = K // KP
GROUPS = M // KP
W1_ROW = 4
X_SPLIT = 320


def tile_mix_dconv_fm_pl_gelu_kernel(
    tc, x, w0_words, w0_scales, w1_words, w1_scales, w2, b, out_0, out_1, out_2
):
    nc = tc.nc
    passes = range(PASSES)
    groups = range(GROUPS)

    with ExitStack() as ctx:
        keep = ctx.enter_context(tc.tile_pool(name="keep", bufs=1))
        stage = ctx.enter_context(tc.tile_pool(name="stage", bufs=4))
        psum = ctx.enter_context(tc.psum_pool(name="psum", bufs=1))
        ctx.enter_context(tc.manual_schedule())

        def tiles(stem, shape, dtype, *counts):
            made = {}
            if len(counts) == 1:
                keys = [(i,) for i in range(counts[0])]
            else:
                keys = [(i, j) for i in range(counts[0]) for j in range(counts[1])]
            for key in keys:
                label = stem + "".join("_%d" % i for i in key)
                made[key] = keep.tile(shape, dtype, name=label, align_bytes=64)
            return made

        x_bf = tiles("x_bf", [P, TX * PACK], BF16, PASSES)
        x_codes = tiles("x_codes", [P, TX], I32, PASSES)
        x_scales = tiles("x_scales", [P, TX], U8, PASSES)
        w0_raw, w1_raw, x_raw = {}, {}, {}
        w0_codes = tiles("w0_codes", [P, 2 * KP], U8, PASSES, GROUPS)
        w1_codes = tiles("w1_codes", [P, KP], I32, PASSES, GROUPS)
        w01_scales = tiles("w01_scales", [P, M], U8, PASSES)
        w2_raw = tiles("w2_raw", [P, PACK, KP], F32, PASSES, GROUPS)
        w2_codes = tiles("w2_codes", [P, KP], I32, PASSES, GROUPS)
        w2_scales = tiles("w2_scales", [P, KP], U8, PASSES, GROUPS)
        y = tiles("y", [P, PACK, T], F32, GROUPS)
        y_bf = tiles("y_bf", [P, T * PACK], BF16, GROUPS)
        y_codes = tiles("y_codes", [P, T], I32, GROUPS)
        y_scales = keep.tile([P, GROUPS, T], U8, name="y_scales", align_bytes=64)
        scales_raw = keep.tile([P, PASSES, M], U8, name="scales_raw", align_bytes=64)
        bias = keep.tile([P, GROUPS, PACK], F32, name="bias")
        w2_bf = {}
        acc = {}

        def load_x(g, lo, hi):
            piece = keep.tile([P, PACK, hi - lo], F32, name="x_raw_%d_%d" % (g, lo), align_bytes=64)
            nc.sync.dma_start(out=piece[:], in_=x[g * KP : (g + 1) * KP, lo:hi].rearrange("(p j) t -> p j t", j=PACK))
            x_raw[g, lo] = piece

        def load_words(held, src, stem, gs, lo, hi):
            width = src.shape[2] // GROUPS
            piece = keep.tile([P, len(gs), width * (hi - lo)], I32, name="%s_%d_%d" % (stem, gs[0], lo), align_bytes=64)
            nc.sync.dma_start(out=piece[:], in_=src[:, gs[0] : gs[-1] + 1, width * lo : width * hi])
            for i, g in enumerate(gs):
                for a in range(lo, hi):
                    held[g, a] = piece[:, i, width * (a - lo) : width * (a - lo + 1)]

        def load_w0(gs, lo, hi):
            load_words(w0_raw, w0_words.bitcast(I32).rearrange("g p c -> p g c"), "w0_raw", gs, lo, hi)

        def load_w1(gs, lo, hi):
            load_words(w1_raw, w1_words.rearrange("g p n i -> p g (n i)").bitcast(I32), "w1_raw", gs, lo, hi)

        def load_w2(g, a):
            rows = w2[g * KP : (g + 1) * KP, a * KP : (a + 1) * KP]
            nc.sync.dma_start(out=w2_raw[g, a][:], in_=rows.rearrange("(p j) n -> p j n", j=PACK))

        def load_scales(*rows):
            for r in rows:
                for src, first in ((w0_scales, 0), (w1_scales, W1_ROW)):
                    nc.sync.dma_start(
                        out=scales_raw[first + r : P : 32, :, :].bitcast(I32),
                        in_=src.rearrange("g (q r) n -> r q g n", r=4)[r].bitcast(I32),
                    )

        nc.vector.memset(scales_raw[:].rearrange("p g n -> p (g n)").bitcast(I32), 0)
        load_w0((0,), 0, 3)
        load_scales(0, 1)
        load_x(0, 0, T)
        load_scales(2, 3)
        load_x(0, T, TX)
        load_w1((0,), 0, 2)
        load_x(1, 0, TX)
        load_w0((1,), 0, 3)
        load_w1((1,), 0, 2)
        nc.sync.dma_start(out=bias[:], in_=b.rearrange("(a p r) -> p a r", a=GROUPS, r=PACK))
        load_w2(0, 0)
        load_w2(1, 0)
        load_w1((0,), 2, 3)
        for a in (1, 2):
            for g in passes:
                load_w2(g, a)
        load_w1((1,), 2, 3)

        def deal_w0(g, a):
            nc.vector.tensor_copy(
                out=w0_codes[g, a][:].rearrange("p (r m c) -> p r m c", r=PACK, c=2),
                in_=w0_raw[g, a].bitcast(U8).rearrange("p (m r c) -> p r m c", r=PACK, c=2),
            )

        def deal_w1(g, a):
            nc.vector.tensor_copy(
                out=w1_codes[g, a][:].rearrange("p (h r m) -> p h m r", h=2, r=2),
                in_=w1_raw[g, a].rearrange("p (m h r) -> p h m r", h=2, r=2),
            )

        def deal_scales(g, lo, hi):
            cols = slice(KP * lo, KP * hi)
            nc.vector.tensor_copy(
                out=w01_scales[g,][:, cols].rearrange("p (a r m) -> p a r m", a=hi - lo, r=PACK),
                in_=scales_raw[:, g, cols].rearrange("p (a m r) -> p a r m", a=hi - lo, r=PACK),
            )

        def interleave(copy, dst, src, lo, hi, first=0):
            copy(
                out=dst[:, PACK * lo : PACK * hi].rearrange("p (c i j) -> p c j i", i=4, j=PACK),
                in_=src[:, :, lo - first : hi - first].rearrange("p j (c i) -> p c j i", i=4),
            )

        def quantize(codes, scales, src, lo, hi):
            nc.vector.quantize_mx(out=codes[:, lo:hi].bitcast(FP8X4), scales=scales[:, lo:hi], in_=src[:, PACK * lo : PACK * hi])

        def cast_x(g):
            interleave(nc.vector.tensor_copy, x_bf[g,], x_raw[g, 0], 0, X_SPLIT)
            interleave(nc.scalar.copy, x_bf[g,], x_raw[g, 0], X_SPLIT, T)
            if g == 0:
                interleave(nc.scalar.copy, x_bf[g,], x_raw[g, T], T, TX, T)
            else:
                interleave(nc.scalar.copy, x_bf[g,], x_raw[g, 0], T, TX)

        def quantize_x(g, lo, hi):
            quantize(x_codes[g,], x_scales[g,], x_bf[g,], lo, hi)

        def cast_w2(copy, g, a, h):
            w2_bf[g, a, h] = stage.tile([P, 2 * KP], BF16, name="w2_bf", align_bytes=64)
            copy(
                out=w2_bf[g, a, h][:].rearrange("p (r m j) -> p m j r", r=2, j=PACK),
                in_=w2_raw[g, a][:].rearrange("p j (m h r) -> p h m j r", h=2, r=2)[:, h, :, :, :],
            )

        def quantize_w2(g, a, h):
            cols = slice(2 * P * h, 2 * P * (h + 1))
            nc.vector.quantize_mx(
                out=w2_codes[g, a][:, cols].bitcast(FP8X4), scales=w2_scales[g, a][:, cols], in_=w2_bf[g, a, h][:]
            )

        def matmul(tap, g, a, r):
            first = tap == 0 and g == 0
            if first:
                acc[a, r] = psum.tile([P, T], F32, name="acc", tag="bank%d" % (PACK * (a % 2) + r))
            cols = slice(P * r, P * (r + 1))
            plane = slice(KP * a + P * r, KP * a + P * (r + 1))
            if tap == 0:
                lhs = w0_codes[g, a][:, 2 * P * r : 2 * P * (r + 1)].bitcast(FP4X4)
                lhs_scale = w01_scales[g,][:, plane]
            elif tap == 1:
                lhs = w1_codes[g, a][:, cols].bitcast(FP8X4)
                lhs_scale = w01_scales[g,][W1_ROW:P, plane]
            else:
                lhs = w2_codes[g, a][:, cols].bitcast(FP8X4)
                lhs_scale = w2_scales[g, a][:, cols]
            window = slice(tap * D, tap * D + T)
            nc.tensor.matmul_mx(
                out=acc[a, r][:],
                lhsT=lhs,
                lhsT_scale=lhs_scale,
                rhs=x_codes[g,][:, window].bitcast(FP8X4),
                rhs_scale=x_scales[g,][:, window],
                start=first,
                stop=(tap == 2 and g == PASSES - 1),
            )

        def matmuls(tap, g, *which):
            for a in which:
                for r in range(PACK):
                    matmul(tap, g, a, r)

        def gelu(a, r, lo, hi):
            nc.scalar.activation(out=y[a,][:, r, lo:hi], in_=acc[a, r][:, lo:hi], func=GELU, bias=bias[:, a, r : r + 1])

        def cast_y(copy, a, lo, hi):
            interleave(copy, y_bf[a,], y[a,], lo, hi)

        def quantize_y(a):
            quantize(y_codes[a,], y_scales[:, a, :], y_bf[a,], 0, T)

        def store_y(a, lo, hi):
            rows = out_0[a * KP : (a + 1) * KP, :].rearrange("(p r) t -> p r t", r=PACK)
            nc.sync.dma_start(out=rows[:, lo:hi, :], in_=y[a,][:, lo:hi, :])

        def store_codes(a):
            nc.sync.dma_start(out=out_1[a].rearrange("p t i -> p (t i)").bitcast(I32), in_=y_codes[a,][:])

        def store_scales():
            for r in range(4):
                nc.scalar.dma_start(
                    out=out_2.rearrange("a (q r) t -> r q a t", r=4)[r].bitcast(I32),
                    in_=y_scales[r:P:32, :, :].bitcast(I32),
                )

        vec, act = nc.vector.tensor_copy, nc.scalar.copy

        for a in groups:
            deal_w0(0, a)
        cast_x(0)
        deal_scales(0, 0, 1)
        quantize_x(0, 0, T)
        matmuls(0, 0, 0)
        deal_scales(0, 1, 2)
        matmuls(0, 0, 1)
        quantize_x(0, T, TX)
        deal_w1(0, 0)
        deal_w1(0, 1)
        matmuls(1, 0, 0, 1)
        deal_scales(1, 0, 3)
        deal_scales(0, 2, 3)

        cast_x(1)
        deal_w0(1, 0)
        quantize_x(1, 0, T)
        deal_w0(1, 1)
        matmuls(0, 1, 0, 1)
        quantize_x(1, T, TX)
        deal_w1(1, 0)
        deal_w1(1, 1)
        matmuls(1, 1, 0, 1)
        deal_w0(1, 2)

        cast_w2(act, 0, 0, 0)
        cast_w2(act, 0, 0, 1)
        quantize_w2(0, 0, 0)
        cast_w2(vec, 1, 0, 0)
        quantize_w2(0, 0, 1)
        matmuls(2, 0, 0)
        cast_w2(vec, 1, 0, 1)
        quantize_w2(1, 0, 0)
        quantize_w2(1, 0, 1)
        matmuls(2, 1, 0)
        deal_w1(0, 2)

        def early_taps(r):
            for tap, g in ((0, 0), (0, 1), (1, 0)):
                matmul(tap, g, 2, r)

        for r in range(PACK):
            gelu(0, r, 0, T)
        store_y(0, 0, PACK)
        for r in range(PACK - 1):
            early_taps(r)

        cast_w2(vec, 0, 1, 0)
        cast_w2(vec, 0, 1, 1)
        quantize_w2(0, 1, 0)
        quantize_w2(0, 1, 1)
        matmuls(2, 0, 1)
        cast_w2(vec, 1, 1, 0)
        cast_w2(act, 1, 1, 1)
        cast_y(vec, 0, 0, 320)
        cast_y(act, 0, 320, T)
        quantize_w2(1, 1, 0)
        quantize_w2(1, 1, 1)
        matmuls(2, 1, 1)
        early_taps(PACK - 1)
        quantize_y(0)
        store_codes(0)
        for r in range(PACK):
            gelu(1, r, 0, T)
        store_y(1, 0, PACK)

        cast_w2(vec, 0, 2, 0)
        cast_w2(vec, 0, 2, 1)
        quantize_w2(0, 2, 0)
        quantize_w2(0, 2, 1)
        matmuls(2, 0, 2)
        cast_w2(vec, 1, 2, 0)
        cast_w2(act, 1, 2, 1)
        deal_w1(1, 2)
        quantize_w2(1, 2, 0)
        quantize_w2(1, 2, 1)
        cast_y(vec, 1, 0, T)
        quantize_y(1)
        for r in range(PACK):
            matmul(1, 1, 2, r)
            matmul(2, 1, 2, r)
            gelu(2, r, 0, T)
            if r == 1:
                store_y(2, 0, 2)
                store_codes(1)
        store_y(2, 2, PACK)
        cast_y(vec, 2, 0, 256)
        cast_y(act, 2, 416, T)
        cast_y(vec, 2, 256, 416)
        quantize(y_codes[2,], y_scales[:, 2, :], y_bf[2,], 0, 256)
        quantize(y_codes[2,], y_scales[:, 2, :], y_bf[2,], 256, T)
        store_codes(2)
        store_scales()
